import numpy as np
import ml_dtypes


def mxq(x, axis, fmt="e4m3"):
    dtype, down = {"e4m3": (ml_dtypes.float8_e4m3fn, 7), "e5m2": (ml_dtypes.float8_e5m2, 14)}[fmt]
    v = np.moveaxis(np.asarray(x, np.float32).astype(ml_dtypes.bfloat16).astype(np.float64), axis, -1)
    blocks = v.reshape(v.shape[:-1] + (-1, 32))
    amax = np.abs(blocks).max(-1, keepdims=True)
    byte = np.maximum(np.where(amax > 0, np.frexp(amax)[1] - 1 + 127, 0) - down, 1)
    scale = np.exp2(byte - 127.0)
    codes = (blocks / scale).astype(np.float32).astype(dtype).astype(np.float64)
    return np.moveaxis((codes * scale).reshape(v.shape), -1, axis)


WIDE = False


def mx_kscale(k):
    if not WIDE:
        return np.ones(k)
    levels = np.array([10, -10, 5, -5, 0])
    if k % 512:
        return np.exp2(np.random.permutation(np.resize(levels, k // 32))).repeat(32)
    a = np.empty((k // 512, 16))
    for p in range(k // 512):
        a[p, :8] = np.random.permutation(np.resize(levels, 8))
        for g in range(8):
            far = levels[np.abs(levels - a[p, g]) >= 10]
            a[p, g + 8] = far[np.random.randint(len(far))]
    return np.exp2(a.ravel()).repeat(32)


def f64(x):
    return np.asarray(x).astype(np.float64)


def striped(idx):
    return np.tile(idx.reshape(-1, 16).T, (8, 1)).astype(np.uint16)


def unstriped(offs):
    return offs[:16].T.reshape(-1).astype(np.int64)


def striped8(idx):
    return np.concatenate([x.reshape(-1, 16).T for x in idx]).astype(np.uint16)


def runs(offs, k):
    lists = np.stack([offs[16 * r : 16 * r + 16].T.reshape(-1) for r in range(8)]).astype(np.int64)
    return lists[np.arange(k) % 512 // 64]


def pack_weight(w):
    k, n = w.shape
    w = f64(np.asarray(w, np.float32).astype(ml_dtypes.bfloat16)).reshape(k // 32, 32, n)
    amax = np.abs(w).max(1)
    byte = np.clip(np.where(amax > 0, np.frexp(amax)[1] - 1 + 127 - 7, 1), 1, 254)
    scaled = (w * np.exp2(127.0 - byte)[:, None, :]).reshape(k, n).astype(np.float32)
    words = np.ascontiguousarray(scaled.reshape(k // 512, 128, 4, n).transpose(0, 1, 3, 2)).astype(ml_dtypes.float8_e4m3fn).view(np.uint8)
    return words, np.ascontiguousarray(byte.astype(np.uint8).reshape(k // 512, 16, n))


def unpack_weight(words, scales):
    g, p, n, _ = words.shape
    vals = np.ascontiguousarray(words).view(ml_dtypes.float8_e4m3fn).astype(np.float64) * np.repeat(np.exp2(scales.astype(np.float64) - 127.0), 8, axis=1)[..., None]
    return vals.transpose(0, 1, 3, 2).reshape(g * 512, n)


def sigmoid(v):
    return 1.0 / (1.0 + np.exp(-np.maximum(v, -700.0)))


K, T, S, N, G, H = 512, 2048, 512, 512, 2048, 512


def setup_inputs():
    n = np.random.standard_normal
    s = mx_kscale(K)[:, None]
    u = mx_kscale(H)
    packed_xT = pack_weight(n((K, T)) * s)
    packed_dT = pack_weight(n((K, G)) / s)
    return {
        "x_words": packed_xT[0],
        "x_scales": packed_xT[1],
        "d_words": packed_dT[0],
        "d_scales": packed_dT[1],
        "gn": (np.random.uniform(0.5, 1.5, (H, 1)) * u[:, None]).astype(np.float32),
        "w1": (n((H, N)) / np.sqrt(H) / u[:, None]).astype(np.float32),
        "offs": striped(np.random.permutation(T)[:S]),
        "k1": striped8(np.random.randint(0, G, (8, H))),
        "k2": striped8(np.random.randint(0, G, (8, H))),
    }


def reference(x_words, x_scales, d_words, d_scales, gn, w1, offs, k1, k2):
    d_k1 = unpack_weight(d_words, d_scales)[np.arange(K)[:, None], runs(k1, K)]
    xq = unpack_weight(x_words, x_scales)[:, unstriped(offs)]
    d_k2 = unpack_weight(d_words, d_scales)[np.arange(K)[:, None], runs(k2, K)]
    s = 0.0625 * ((d_k1.T @ xq) + 0.5 * (d_k2.T @ xq))
    z = f64(gn) * sigmoid(s)
    return mxq(f64(w1), 0, "e4m3").T @ mxq(z, 0, "e4m3")

@@ -1,0 +1,163 @@
+from contextlib import ExitStack
+
+import concourse.mybir as mybir
+
+K, T, S, N, G, H = 512, 2048, 512, 512, 2048, 512
+FLOPS = 2 * K * H * S * 2 + 2 * H * N * S
+
+F32 = mybir.dt.float32
+BF16 = mybir.dt.bfloat16
+I32 = mybir.dt.int32
+U32 = mybir.dt.uint32
+U16 = mybir.dt.uint16
+U8 = mybir.dt.uint8
+FP8X4 = mybir.dt.float8_e4m3fn_x4
+MULT = mybir.AluOpType.mult
+ADD = mybir.AluOpType.add
+SIGMOID = mybir.ActivationFunctionType.Sigmoid
+
+P = 128
+PACK = 4
+CHUNK = 128
+HALF = 256
+
+
+def tile_picked_rpqscore_sigmoid_p_kernel(
+    tc, x_words, x_scales, d_words, d_scales, gn, w1, offs, k1, k2, out
+):
+    nc = tc.nc
+    with ExitStack() as ctx:
+        sb = ctx.enter_context(tc.tile_pool(name="sb", bufs=1))
+        ps = ctx.enter_context(tc.psum_pool(name="ps", bufs=1))
+
+        def mm(acc, lw, ls, rw, rs, start, stop):
+            nc.tensor.matmul_mx(out=acc, lhsT=lw.bitcast(FP8X4), lhsT_scale=ls, rhs=rw.bitcast(FP8X4), rhs_scale=rs, start=start, stop=stop)
+
+        k1_t = sb.tile([P, H // 16], U16, name="k1_t")
+        k2_t = sb.tile([P, H // 16], U16, name="k2_t")
+        offs_t = sb.tile([P, S // 16], U16, name="offs_t")
+        d_tab = sb.tile([P, G], I32, name="d_tab", align_bytes=64)
+        x_tab = sb.tile([P, T], I32, name="x_tab", align_bytes=64)
+        ds_tab = sb.tile([P, G], U8, name="ds_tab", align_bytes=64)
+        xs_tab = sb.tile([P, T], U8, name="xs_tab", align_bytes=64)
+        gn_t = sb.tile([P, PACK], F32, name="gn_t")
+        w_raw = [sb.tile([P, PACK, HALF], F32, name="w_raw%d" % h, align_bytes=64) for h in range(2)]
+
+        w_rows = w1.rearrange("(p t) n -> p t n", t=PACK)
+        nc.sync.dma_start(k1_t[:], k1)
+        nc.sync.dma_start(ds_tab[:].bitcast(I32), d_scales[0].bitcast(I32).unsqueeze(1).to_broadcast([16, 8, G // 4]))
+        nc.sync.dma_start(k2_t[:], k2)
+        nc.sync.dma_start(x_tab[:], x_words[0].rearrange("p n t -> p (n t)").bitcast(I32))
+        nc.sync.dma_start(offs_t[:], offs)
+        for q in range(4):
+            nc.sync.dma_start(
+                xs_tab[32 * q : 32 * q + 32, :].bitcast(I32),
+                x_scales[0, 4 * q : 4 * q + 4, :].bitcast(I32).unsqueeze(0).to_broadcast([8, 4, T // 4]),
+            )
+        nc.sync.dma_start(d_tab[:], d_words[0].rearrange("p n t -> p (n t)").bitcast(I32))
+        nc.sync.dma_start(w_raw[0][:], w_rows[:, :, 0:HALF])
+        nc.sync.dma_start(w_raw[1][:], w_rows[:, :, HALF:N])
+        nc.sync.dma_start(gn_t[:], gn.rearrange("(p t) o -> p (t o)", t=PACK))
+
+        warm_in = sb.tile([P, 1], F32, name="warm_in")
+        warm_out = sb.tile([P, 1], F32, name="warm_out")
+        nc.vector.memset(warm_in[:], 0.0)
+        nc.scalar.activation(warm_out[:], warm_in[:], SIGMOID)
+
+        ds_got = sb.tile([P, 2 * H], U8, name="ds_got", align_bytes=64)
+        nc.vector.tensor_copy(ds_got[:, 0:H], ds_tab[:].indirect(k1_t[:]))
+        nc.vector.tensor_copy(ds_got[:, H : 2 * H], ds_tab[:].indirect(k2_t[:]))
+        ds_key = sb.tile([P, 2 * H], U8, name="ds_key", align_bytes=64)
+        nc.vector.tensor_copy(
+            ds_key[:].rearrange("p (a t m) -> p a t m", a=2, t=PACK),
+            ds_got[:].rearrange("p (a m t) -> p a t m", a=2, t=PACK),
+        )
+        for r in range(1, 4):
+            nc.scalar.dma_start(ds_key[r:P:32, :].bitcast(I32), ds_key[8 * r : P : 32, :].bitcast(I32))
+
+        d_got = [sb.tile([P, H], U32, name="d_got%d" % a, tag="reuse%d" % a, align_bytes=64) for a in range(2)]
+        xs_got = [sb.tile([P, HALF], U8, name="xs_got%d" % h, tag=("xs_first", "reuse0")[h], align_bytes=64) for h in range(2)]
+        x_got = [sb.tile([P, HALF], U32, name="x_got%d" % h, tag=("x_first", "reuse1")[h], align_bytes=64) for h in range(2)]
+        d_key = [sb.tile([P, H], U32, name="d_key%d" % a, align_bytes=64) for a in range(2)]
+
+        def pick_tokens_scales(h):
+            nc.vector.tensor_copy(xs_got[h][:], xs_tab[:].indirect(offs_t[:, 16 * h : 16 * h + 16]))
+
+        def pick_tokens_words(h):
+            nc.vector.tensor_copy(x_got[h][:], x_tab[:].bitcast(U32).indirect(offs_t[:, 16 * h : 16 * h + 16]))
+
+        def pick_codes(a, lst):
+            nc.vector.tensor_copy(d_got[a][:], d_tab[:].bitcast(U32).indirect(lst[:]))
+            nc.vector.tensor_copy(
+                d_key[a][:].rearrange("p (t m) -> p m t", t=PACK),
+                d_got[a][:].rearrange("p (m t) -> p m t", t=PACK),
+            )
+
+        w_bf = [sb.tile([P, HALF * PACK], BF16, name="w_bf%d" % h, align_bytes=64) for h in range(2)]
+        w_q = [sb.tile([P, HALF], U32, name="w_q%d" % h, align_bytes=64) for h in range(2)]
+        w_s = [sb.tile([P, HALF], U8, name="w_s%d" % h, align_bytes=64) for h in range(2)]
+
+        def cast_w(h):
+            nc.scalar.copy(
+                w_bf[h][:].rearrange("p (c i t) -> p c t i", i=4, t=PACK),
+                w_raw[h][:].rearrange("p t (c i) -> p c t i", i=4),
+            )
+
+        def quant_w(h):
+            nc.vector.quantize_mx(out=w_q[h][:].bitcast(FP8X4), scales=w_s[h][:], in_=w_bf[h][:])
+
+        def score(acc, t, a, c, start, stop):
+            h, o = divmod(c * CHUNK, HALF)
+            mm(acc[:, t, :], d_key[a][:, t * P : (t + 1) * P], ds_key[:, a * H + t * P : a * H + (t + 1) * P],
+               x_got[h][:, o : o + CHUNK], xs_got[h][:, o : o + CHUNK], start, stop)
+
+        pick_tokens_scales(0)
+        pick_tokens_words(0)
+        pick_codes(0, k1_t)
+        cast_w(0)
+
+        first_a = ps.tile([P, PACK, CHUNK], F32, name="first_a")
+        first_b = ps.tile([P, PACK, CHUNK], F32, name="first_b")
+        for t in range(PACK):
+            score(first_a, t, 0, 0, True, True)
+        a_sb = sb.tile([P, CHUNK, PACK], F32, name="a_sb")
+        nc.scalar.copy(a_sb[:], first_a[:].rearrange("p t n -> p n t"))
+
+        pick_codes(1, k2_t)
+        cast_w(1)
+        for t in range(PACK):
+            score(first_b, t, 1, 0, True, True)
+        pick_tokens_scales(1)
+        pick_tokens_words(1)
+        s_sb = sb.tile([P, CHUNK, PACK], F32, name="s_sb")
+        nc.vector.scalar_tensor_tensor(s_sb[:], first_b[:].rearrange("p t n -> p n t"), 0.5, a_sb[:], MULT, ADD)
+        quant_w(0)
+        quant_w(1)
+
+        sig = [sb.tile([P, CHUNK, PACK], F32, name="sig%d" % c) for c in range(4)]
+        nc.scalar.activation(sig[0][:], s_sb[:], SIGMOID, scale=0.0625)
+        for c in range(1, 4):
+            acc = ps.tile([P, PACK, CHUNK], F32, name="acc%d" % c)
+            for t in range(PACK):
+                score(acc, t, 0, c, True, False)
+                score(acc, t, 0, c, False, False)
+                score(acc, t, 1, c, False, True)
+            nc.scalar.activation(sig[c][:], acc[:].rearrange("p t n -> p n t"), SIGMOID, scale=0.03125)
+
+        out_rows = out.rearrange("(u p) n -> p u n", p=P)
+        for c in range(4):
+            z_bf = sb.tile([P, CHUNK, PACK], BF16, name="z_bf%d" % c, align_bytes=64)
+            nc.vector.tensor_tensor(z_bf[:], sig[c][:], gn_t[:].unsqueeze(1).to_broadcast([P, CHUNK, PACK]), MULT)
+            z_q = sb.tile([P, CHUNK], U32, name="z_q%d" % c, align_bytes=64)
+            z_s = sb.tile([P, CHUNK], U8, name="z_s%d" % c, align_bytes=64)
+            nc.vector.quantize_mx(out=z_q[:].bitcast(FP8X4), scales=z_s[:], in_=z_bf[:].rearrange("p n t -> p (n t)"))
+            res = ps.tile([P, PACK, CHUNK], F32, name="res", tag="res", bufs=3)
+            for u in range(4):
+                h, o = divmod(u * P, HALF)
+                mm(res[:, u, :], w_q[h][:, o : o + P], w_s[h][:, o : o + P], z_q[:], z_s[:], True, True)
+            res_sb = sb.tile([P, PACK, CHUNK], F32, name="res_sb%d" % c)
+            if c < 3:
+                nc.scalar.copy(res_sb[:], res[:])
+            else:
+                nc.vector.tensor_copy(res_sb[:], res[:])
+            nc.sync.dma_start(out_rows[:, :, c * CHUNK : (c + 1) * CHUNK], res_sb[:])

@@ -41,123 +41,138 @@ def tile_picked_rpqscore_sigmoid_p_kernel(
         ds_tab = sb.tile([P, G], U8, name="ds_tab", align_bytes=64)
         xs_tab = sb.tile([P, T], U8, name="xs_tab", align_bytes=64)
         gn_t = sb.tile([P, PACK], F32, name="gn_t")
-        w_raw = [sb.tile([P, PACK, HALF], F32, name="w_raw%d" % h, align_bytes=64) for h in range(2)]
-
-        w_rows = w1.rearrange("(p t) n -> p t n", t=PACK)
-        nc.sync.dma_start(k1_t[:], k1)
-        nc.sync.dma_start(ds_tab[:].bitcast(I32), d_scales[0].bitcast(I32).unsqueeze(1).to_broadcast([16, 8, G // 4]))
-        nc.sync.dma_start(k2_t[:], k2)
-        nc.sync.dma_start(x_tab[:], x_words[0].rearrange("p n t -> p (n t)").bitcast(I32))
-        nc.sync.dma_start(offs_t[:], offs)
-        for q in range(4):
-            nc.sync.dma_start(
-                xs_tab[32 * q : 32 * q + 32, :].bitcast(I32),
-                x_scales[0, 4 * q : 4 * q + 4, :].bitcast(I32).unsqueeze(0).to_broadcast([8, 4, T // 4]),
-            )
-        nc.sync.dma_start(d_tab[:], d_words[0].rearrange("p n t -> p (n t)").bitcast(I32))
-        nc.sync.dma_start(w_raw[0][:], w_rows[:, :, 0:HALF])
-        nc.sync.dma_start(w_raw[1][:], w_rows[:, :, HALF:N])
-        nc.sync.dma_start(gn_t[:], gn.rearrange("(p t) o -> p (t o)", t=PACK))
+        w_raw = sb.tile([P, 2, PACK, HALF], F32, name="w_raw", tag="slot_b", align_bytes=64)
 
         warm_in = sb.tile([P, 1], F32, name="warm_in")
         warm_out = sb.tile([P, 1], F32, name="warm_out")
-        nc.vector.memset(warm_in[:], 0.0)
+        nc.vector.memset(ds_tab[:].bitcast(I32), 0)
+        nc.vector.memset(xs_tab[:].bitcast(I32), 0)
+        nc.gpsimd.memset(warm_in[:], 0.0)
         nc.scalar.activation(warm_out[:], warm_in[:], SIGMOID)
 
+        w_rows = w1.rearrange("(p t) n -> p t n", t=PACK)
+        nc.sync.dma_start(ds_tab[0:P:8, :].bitcast(I32), d_scales[0].bitcast(I32))
+        nc.sync.dma_start(xs_tab[0:P:8, :].bitcast(I32), x_scales[0].bitcast(I32))
+        nc.sync.dma_start(k1_t[:], k1)
+        nc.sync.dma_start(k2_t[:], k2)
+        nc.sync.dma_start(offs_t[:], offs)
+        nc.sync.dma_start(gn_t[:], gn.rearrange("(p t) o -> p (t o)", t=PACK))
+        nc.sync.dma_start(x_tab[:], x_words[0].rearrange("p n t -> p (n t)").bitcast(I32))
+        nc.sync.dma_start(d_tab[:], d_words[0].rearrange("p n t -> p (n t)").bitcast(I32))
+        for h in range(2):
+            nc.sync.dma_start(w_raw[:, h], w_rows[:, :, h * HALF : (h + 1) * HALF])
+
         ds_got = sb.tile([P, 2 * H], U8, name="ds_got", align_bytes=64)
+        xs_got = sb.tile([P, S], U8, name="xs_got", align_bytes=64)
         nc.vector.tensor_copy(ds_got[:, 0:H], ds_tab[:].indirect(k1_t[:]))
         nc.vector.tensor_copy(ds_got[:, H : 2 * H], ds_tab[:].indirect(k2_t[:]))
-        ds_key = sb.tile([P, 2 * H], U8, name="ds_key", align_bytes=64)
+        nc.vector.tensor_copy(xs_got[:], xs_tab[:].indirect(offs_t[:]))
+        planes = sb.tile([P, 2 * H + S], U8, name="planes", align_bytes=64)
         nc.vector.tensor_copy(
-            ds_key[:].rearrange("p (a t m) -> p a t m", a=2, t=PACK),
+            planes[:, 0 : 2 * H].rearrange("p (a t m) -> p a t m", a=2, t=PACK),
             ds_got[:].rearrange("p (a m t) -> p a t m", a=2, t=PACK),
         )
+        nc.vector.tensor_copy(planes[:, 2 * H :].bitcast(I32), xs_got[:].bitcast(I32))
         for r in range(1, 4):
-            nc.scalar.dma_start(ds_key[r:P:32, :].bitcast(I32), ds_key[8 * r : P : 32, :].bitcast(I32))
+            nc.sync.dma_start(planes[r:P:32, :].bitcast(I32), planes[8 * r : P : 32, :].bitcast(I32))
 
-        d_got = [sb.tile([P, H], U32, name="d_got%d" % a, tag="reuse%d" % a, align_bytes=64) for a in range(2)]
-        xs_got = [sb.tile([P, HALF], U8, name="xs_got%d" % h, tag=("xs_first", "reuse0")[h], align_bytes=64) for h in range(2)]
-        x_got = [sb.tile([P, HALF], U32, name="x_got%d" % h, tag=("x_first", "reuse1")[h], align_bytes=64) for h in range(2)]
         d_key = [sb.tile([P, H], U32, name="d_key%d" % a, align_bytes=64) for a in range(2)]
+        w_bf = sb.tile([P, N * PACK], BF16, name="w_bf", align_bytes=64)
+        w_s = sb.tile([P, N], U8, name="w_s", align_bytes=64)
 
-        def pick_tokens_scales(h):
-            nc.vector.tensor_copy(xs_got[h][:], xs_tab[:].indirect(offs_t[:, 16 * h : 16 * h + 16]))
+        def pick_token_words(h, tag):
+            got = sb.tile([P, HALF], U32, name="x_got%d" % h, tag=tag, align_bytes=64)
+            nc.vector.tensor_copy(got[:], x_tab[:].bitcast(U32).indirect(offs_t[:, 16 * h : 16 * h + 16]))
+            return got
 
-        def pick_tokens_words(h):
-            nc.vector.tensor_copy(x_got[h][:], x_tab[:].bitcast(U32).indirect(offs_t[:, 16 * h : 16 * h + 16]))
-
-        def pick_codes(a, lst):
-            nc.vector.tensor_copy(d_got[a][:], d_tab[:].bitcast(U32).indirect(lst[:]))
+        def pick_codes(a, lst, tag):
+            got = sb.tile([P, H], U32, name="d_got%d" % a, tag=tag, align_bytes=64)
+            nc.vector.tensor_copy(got[:], d_tab[:].bitcast(U32).indirect(lst[:]))
             nc.vector.tensor_copy(
                 d_key[a][:].rearrange("p (t m) -> p m t", t=PACK),
-                d_got[a][:].rearrange("p (m t) -> p m t", t=PACK),
+                got[:].rearrange("p (m t) -> p m t", t=PACK),
             )
 
-        w_bf = [sb.tile([P, HALF * PACK], BF16, name="w_bf%d" % h, align_bytes=64) for h in range(2)]
-        w_q = [sb.tile([P, HALF], U32, name="w_q%d" % h, align_bytes=64) for h in range(2)]
-        w_s = [sb.tile([P, HALF], U8, name="w_s%d" % h, align_bytes=64) for h in range(2)]
+        def score(acc, t, a, h, start, stop):
+            mm(acc, d_key[a][:, t * P : (t + 1) * P], planes[:, a * H + t * P : a * H + (t + 1) * P],
+               x_got[h][:], planes[:, 2 * H + h * HALF : 2 * H + (h + 1) * HALF], start, stop)
 
         def cast_w(h):
             nc.scalar.copy(
-                w_bf[h][:].rearrange("p (c i t) -> p c t i", i=4, t=PACK),
-                w_raw[h][:].rearrange("p t (c i) -> p c t i", i=4),
+                w_bf[:, h * HALF * PACK : (h + 1) * HALF * PACK].rearrange("p (c i t) -> p c t i", i=4, t=PACK),
+                w_raw[:, h].rearrange("p t (c i) -> p c t i", i=4),
             )
 
-        def quant_w(h):
-            nc.vector.quantize_mx(out=w_q[h][:].bitcast(FP8X4), scales=w_s[h][:], in_=w_bf[h][:])
-
-        def score(acc, t, a, c, start, stop):
-            h, o = divmod(c * CHUNK, HALF)
-            mm(acc[:, t, :], d_key[a][:, t * P : (t + 1) * P], ds_key[:, a * H + t * P : a * H + (t + 1) * P],
-               x_got[h][:, o : o + CHUNK], xs_got[h][:, o : o + CHUNK], start, stop)
-
-        pick_tokens_scales(0)
-        pick_tokens_words(0)
-        pick_codes(0, k1_t)
+        x_got = [pick_token_words(0, "x_first")]
+        pick_codes(0, k1_t, "slot_d")
         cast_w(0)
-
-        first_a = ps.tile([P, PACK, CHUNK], F32, name="first_a")
-        first_b = ps.tile([P, PACK, CHUNK], F32, name="first_b")
-        for t in range(PACK):
-            score(first_a, t, 0, 0, True, True)
-        a_sb = sb.tile([P, CHUNK, PACK], F32, name="a_sb")
-        nc.scalar.copy(a_sb[:], first_a[:].rearrange("p t n -> p n t"))
-
-        pick_codes(1, k2_t)
         cast_w(1)
-        for t in range(PACK):
-            score(first_b, t, 1, 0, True, True)
-        pick_tokens_scales(1)
-        pick_tokens_words(1)
-        s_sb = sb.tile([P, CHUNK, PACK], F32, name="s_sb")
-        nc.vector.scalar_tensor_tensor(s_sb[:], first_b[:].rearrange("p t n -> p n t"), 0.5, a_sb[:], MULT, ADD)
-        quant_w(0)
-        quant_w(1)
 
-        sig = [sb.tile([P, CHUNK, PACK], F32, name="sig%d" % c) for c in range(4)]
-        nc.scalar.activation(sig[0][:], s_sb[:], SIGMOID, scale=0.0625)
-        for c in range(1, 4):
-            acc = ps.tile([P, PACK, CHUNK], F32, name="acc%d" % c)
-            for t in range(PACK):
-                score(acc, t, 0, c, True, False)
-                score(acc, t, 0, c, False, False)
-                score(acc, t, 1, c, False, True)
-            nc.scalar.activation(sig[c][:], acc[:].rearrange("p t n -> p n t"), SIGMOID, scale=0.03125)
+        lone_a = ps.tile([P, 2, HALF], F32, name="lone_a", tag="bank0")
+        lone_b = ps.tile([P, 2, HALF], F32, name="lone_b", tag="bank1")
+        early = [ps.tile([P, HALF], F32, name="early%d" % t, tag="bank%d" % (2 + t)) for t in range(2)]
+        late = [ps.tile([P, 2, HALF], F32, name="late%d" % v, tag="bank%d" % (4 + v)) for v in range(2)]
+        for t in range(2):
+            score(lone_a[:, t, :], 2 + t, 0, 0, True, True)
+        for t in range(2):
+            score(early[t][:], t, 0, 0, True, False)
+            score(early[t][:], t, 0, 0, False, False)
+        a_sb = sb.tile([P, 2 * HALF], F32, name="a_sb", tag="slot_b", align_bytes=64)
+        nc.scalar.copy(a_sb[:], lone_a[:].rearrange("p t n -> p (t n)"))
+
+        pick_codes(1, k2_t, "slot_d")
+        for t in range(2):
+            score(lone_b[:, t, :], 2 + t, 1, 0, True, True)
+        for t in range(2):
+            score(early[t][:], t, 1, 0, False, True)
+        x_got.append(pick_token_words(1, "slot_d"))
+        for t in range(PACK):
+            score(late[t // 2][:, t % 2, :], t, 0, 1, True, False)
+            score(late[t // 2][:, t % 2, :], t, 0, 1, False, False)
+            score(late[t // 2][:, t % 2, :], t, 1, 1, False, True)
+
+        s_sb = sb.tile([P, 2 * HALF], F32, name="s_sb", tag="slot_s", align_bytes=64)
+        nc.vector.scalar_tensor_tensor(s_sb[:], lone_b[:].rearrange("p t n -> p (t n)"), 0.5, a_sb[:], MULT, ADD)
+        w_q = sb.tile([P, N], U32, name="w_q", tag="slot_b", align_bytes=64)
+        nc.vector.quantize_mx(out=w_q[:].bitcast(FP8X4), scales=w_s[:], in_=w_bf[:])
+
+        sig0 = sb.tile([P, PACK, HALF], F32, name="sig0")
+        for t in range(2):
+            nc.scalar.activation(sig0[:, t, :], early[t][:], SIGMOID, scale=0.03125)
+        nc.scalar.activation(sig0[:, 2:4, :].rearrange("p t n -> p (t n)"), s_sb[:], SIGMOID, scale=0.0625)
+        sig1 = sb.tile([P, PACK, HALF], F32, name="sig1", tag="slot_s", align_bytes=64)
+        for v in range(2):
+            nc.scalar.activation(sig1[:, 2 * v : 2 * v + 2, :], late[v][:], SIGMOID, scale=0.03125)
+        sig = [sig0, sig1]
 
         out_rows = out.rearrange("(u p) n -> p u n", p=P)
+        gate = gn_t[:].unsqueeze(1).unsqueeze(3).to_broadcast([P, CHUNK // 4, PACK, 4])
+        bank = 0
         for c in range(4):
-            z_bf = sb.tile([P, CHUNK, PACK], BF16, name="z_bf%d" % c, align_bytes=64)
-            nc.vector.tensor_tensor(z_bf[:], sig[c][:], gn_t[:].unsqueeze(1).to_broadcast([P, CHUNK, PACK]), MULT)
+            h, o = divmod(c * CHUNK, HALF)
+            z_bf = sb.tile([P, CHUNK * PACK], BF16, name="z_bf%d" % c, tag="z_bf", bufs=2, align_bytes=64)
+            nc.vector.tensor_tensor(
+                z_bf[:].rearrange("p (c i t) -> p c t i", i=4, t=PACK),
+                sig[h][:, :, o : o + CHUNK].rearrange("p t (c i) -> p c t i", i=4),
+                gate,
+                MULT,
+            )
             z_q = sb.tile([P, CHUNK], U32, name="z_q%d" % c, align_bytes=64)
             z_s = sb.tile([P, CHUNK], U8, name="z_s%d" % c, align_bytes=64)
-            nc.vector.quantize_mx(out=z_q[:].bitcast(FP8X4), scales=z_s[:], in_=z_bf[:].rearrange("p n t -> p (n t)"))
-            res = ps.tile([P, PACK, CHUNK], F32, name="res", tag="res", bufs=3)
-            for u in range(4):
-                h, o = divmod(u * P, HALF)
-                mm(res[:, u, :], w_q[h][:, o : o + P], w_s[h][:, o : o + P], z_q[:], z_s[:], True, True)
-            res_sb = sb.tile([P, PACK, CHUNK], F32, name="res_sb%d" % c)
-            if c < 3:
-                nc.scalar.copy(res_sb[:], res[:])
-            else:
-                nc.vector.tensor_copy(res_sb[:], res[:])
-            nc.sync.dma_start(out_rows[:, :, c * CHUNK : (c + 1) * CHUNK], res_sb[:])
+            nc.vector.quantize_mx(out=z_q[:].bitcast(FP8X4), scales=z_s[:], in_=z_bf[:])
+            parts = 1 + h
+            per = 4 // parts
+            for part in range(parts):
+                res = ps.tile([P, per, CHUNK], F32, name="res%d_%d" % (c, part), tag="bank%d" % bank)
+                bank = bank + 1
+                for v in range(per):
+                    u = part * per + v
+                    mm(res[:, v, :], w_q[:, u * P : (u + 1) * P], w_s[:, u * P : (u + 1) * P], z_q[:], z_s[:], True, True)
+                res_sb = sb.tile([P, per, CHUNK], F32, name="res_sb%d_%d" % (c, part))
+                dst = out_rows[:, part * per : (part + 1) * per, c * CHUNK : (c + 1) * CHUNK]
+                if part == 0:
+                    nc.scalar.copy(res_sb[:], res[:])
+                    (nc.scalar if c == 3 else nc.sync).dma_start(dst, res_sb[:])
+                else:
+                    nc.vector.tensor_copy(res_sb[:], res[:])
+                    nc.sync.dma_start(dst, res_sb[:])

@@ -41,7 +41,7 @@ def tile_picked_rpqscore_sigmoid_p_kernel(
         ds_tab = sb.tile([P, G], U8, name="ds_tab", align_bytes=64)
         xs_tab = sb.tile([P, T], U8, name="xs_tab", align_bytes=64)
         gn_t = sb.tile([P, PACK], F32, name="gn_t")
-        w_raw = sb.tile([P, 2, PACK, HALF], F32, name="w_raw", tag="slot_b", align_bytes=64)
+        w_raw = [sb.tile([P, PACK, HALF], F32, name="w_raw%d" % h, tag=("w_first", "slot_b")[h], align_bytes=64) for h in range(2)]
 
         warm_in = sb.tile([P, 1], F32, name="warm_in")
         warm_out = sb.tile([P, 1], F32, name="warm_out")
@@ -60,18 +60,19 @@ def tile_picked_rpqscore_sigmoid_p_kernel(
         nc.sync.dma_start(x_tab[:], x_words[0].rearrange("p n t -> p (n t)").bitcast(I32))
         nc.sync.dma_start(d_tab[:], d_words[0].rearrange("p n t -> p (n t)").bitcast(I32))
         for h in range(2):
-            nc.sync.dma_start(w_raw[:, h], w_rows[:, :, h * HALF : (h + 1) * HALF])
+            nc.sync.dma_start(w_raw[h][:], w_rows[:, :, h * HALF : (h + 1) * HALF])
 
         ds_got = sb.tile([P, 2 * H], U8, name="ds_got", align_bytes=64)
-        xs_got = sb.tile([P, S], U8, name="xs_got", align_bytes=64)
+        xs_got = sb.tile([P, S], U8, name="xs_got", tag="x_first", align_bytes=64)
         nc.vector.tensor_copy(ds_got[:, 0:H], ds_tab[:].indirect(k1_t[:]))
         nc.vector.tensor_copy(ds_got[:, H : 2 * H], ds_tab[:].indirect(k2_t[:]))
         nc.vector.tensor_copy(xs_got[:], xs_tab[:].indirect(offs_t[:]))
         planes = sb.tile([P, 2 * H + S], U8, name="planes", align_bytes=64)
-        nc.vector.tensor_copy(
-            planes[:, 0 : 2 * H].rearrange("p (a t m) -> p a t m", a=2, t=PACK),
-            ds_got[:].rearrange("p (a m t) -> p a t m", a=2, t=PACK),
-        )
+        for a in range(2):
+            nc.vector.tensor_copy(
+                planes[:, a * H : (a + 1) * H].rearrange("p (t m) -> p t m", t=PACK),
+                ds_got[:, a * H : (a + 1) * H].rearrange("p (m t) -> p t m", t=PACK),
+            )
         nc.vector.tensor_copy(planes[:, 2 * H :].bitcast(I32), xs_got[:].bitcast(I32))
         for r in range(1, 4):
             nc.sync.dma_start(planes[r:P:32, :].bitcast(I32), planes[8 * r : P : 32, :].bitcast(I32))
@@ -85,13 +86,15 @@ def tile_picked_rpqscore_sigmoid_p_kernel(
             nc.vector.tensor_copy(got[:], x_tab[:].bitcast(U32).indirect(offs_t[:, 16 * h : 16 * h + 16]))
             return got
 
-        def pick_codes(a, lst, tag):
-            got = sb.tile([P, H], U32, name="d_got%d" % a, tag=tag, align_bytes=64)
-            nc.vector.tensor_copy(got[:], d_tab[:].bitcast(U32).indirect(lst[:]))
-            nc.vector.tensor_copy(
-                d_key[a][:].rearrange("p (t m) -> p m t", t=PACK),
-                got[:].rearrange("p (m t) -> p m t", t=PACK),
-            )
+        def pick_codes(a, lst):
+            got = [sb.tile([P, HALF], U32, name="d_got%d_%d" % (a, h), tag="slot_d%d" % h, align_bytes=64) for h in range(2)]
+            for h in range(2):
+                nc.vector.tensor_copy(got[h][:], d_tab[:].bitcast(U32).indirect(lst[:, 16 * h : 16 * h + 16]))
+            for h in range(2):
+                nc.vector.tensor_copy(
+                    d_key[a][:].rearrange("p (t m) -> p m t", t=PACK)[:, 64 * h : 64 * h + 64, :],
+                    got[h][:].rearrange("p (m t) -> p m t", t=PACK),
+                )
 
         def score(acc, t, a, h, start, stop):
             mm(acc, d_key[a][:, t * P : (t + 1) * P], planes[:, a * H + t * P : a * H + (t + 1) * P],
@@ -100,11 +103,11 @@ def tile_picked_rpqscore_sigmoid_p_kernel(
         def cast_w(h):
             nc.scalar.copy(
                 w_bf[:, h * HALF * PACK : (h + 1) * HALF * PACK].rearrange("p (c i t) -> p c t i", i=4, t=PACK),
-                w_raw[:, h].rearrange("p t (c i) -> p c t i", i=4),
+                w_raw[h][:].rearrange("p t (c i) -> p c t i", i=4),
             )
 
         x_got = [pick_token_words(0, "x_first")]
-        pick_codes(0, k1_t, "slot_d")
+        pick_codes(0, k1_t)
         cast_w(0)
         cast_w(1)
 
@@ -120,12 +123,12 @@ def tile_picked_rpqscore_sigmoid_p_kernel(
         a_sb = sb.tile([P, 2 * HALF], F32, name="a_sb", tag="slot_b", align_bytes=64)
         nc.scalar.copy(a_sb[:], lone_a[:].rearrange("p t n -> p (t n)"))
 
-        pick_codes(1, k2_t, "slot_d")
+        pick_codes(1, k2_t)
         for t in range(2):
             score(lone_b[:, t, :], 2 + t, 1, 0, True, True)
         for t in range(2):
             score(early[t][:], t, 1, 0, False, True)
-        x_got.append(pick_token_words(1, "slot_d"))
+        x_got.append(pick_token_words(1, "slot_d0"))
         for t in range(PACK):
             score(late[t // 2][:, t % 2, :], t, 0, 1, True, False)
             score(late[t // 2][:, t % 2, :], t, 0, 1, False, False)

from contextlib import ExitStack

import concourse.mybir as mybir

K, T, S, N, G, H = 512, 2048, 512, 512, 2048, 512
FLOPS = 2 * K * H * S * 2 + 2 * H * N * S

F32 = mybir.dt.float32
BF16 = mybir.dt.bfloat16
I32 = mybir.dt.int32
U32 = mybir.dt.uint32
U16 = mybir.dt.uint16
U8 = mybir.dt.uint8
FP8X4 = mybir.dt.float8_e4m3fn_x4
MULT = mybir.AluOpType.mult
ADD = mybir.AluOpType.add
SIGMOID = mybir.ActivationFunctionType.Sigmoid

P = 128
PACK = 4
CHUNK = 128
HALF = 256


def tile_picked_rpqscore_sigmoid_p_kernel(
    tc, x_words, x_scales, d_words, d_scales, gn, w1, offs, k1, k2, out
):
    nc = tc.nc
    with ExitStack() as ctx:
        sb = ctx.enter_context(tc.tile_pool(name="sb", bufs=1))
        ps = ctx.enter_context(tc.psum_pool(name="ps", bufs=1))

        def mm(acc, lw, ls, rw, rs, start, stop):
            nc.tensor.matmul_mx(out=acc, lhsT=lw.bitcast(FP8X4), lhsT_scale=ls, rhs=rw.bitcast(FP8X4), rhs_scale=rs, start=start, stop=stop)

        k1_t = sb.tile([P, H // 16], U16, name="k1_t")
        k2_t = sb.tile([P, H // 16], U16, name="k2_t")
        offs_t = sb.tile([P, S // 16], U16, name="offs_t")
        d_tab = sb.tile([P, G], I32, name="d_tab", align_bytes=64)
        x_tab = sb.tile([P, T], I32, name="x_tab", align_bytes=64)
        ds_tab = sb.tile([P, G], U8, name="ds_tab", align_bytes=64)
        xs_tab = sb.tile([P, T], U8, name="xs_tab", align_bytes=64)
        gn_t = sb.tile([P, PACK], F32, name="gn_t")
        w_raw = [sb.tile([P, PACK, HALF], F32, name="w_raw%d" % h, tag=("w_first", "slot_b")[h], align_bytes=64) for h in range(2)]

        warm_in = sb.tile([P, 1], F32, name="warm_in")
        warm_out = sb.tile([P, 1], F32, name="warm_out")
        nc.vector.memset(ds_tab[:].bitcast(I32), 0)
        nc.vector.memset(xs_tab[:].bitcast(I32), 0)
        nc.gpsimd.memset(warm_in[:], 0.0)
        nc.scalar.activation(warm_out[:], warm_in[:], SIGMOID)

        w_rows = w1.rearrange("(p t) n -> p t n", t=PACK)
        nc.sync.dma_start(ds_tab[0:P:8, :].bitcast(I32), d_scales[0].bitcast(I32))
        nc.sync.dma_start(xs_tab[0:P:8, :].bitcast(I32), x_scales[0].bitcast(I32))
        nc.sync.dma_start(k1_t[:], k1)
        nc.sync.dma_start(k2_t[:], k2)
        nc.sync.dma_start(offs_t[:], offs)
        nc.sync.dma_start(gn_t[:], gn.rearrange("(p t) o -> p (t o)", t=PACK))
        nc.sync.dma_start(x_tab[:], x_words[0].rearrange("p n t -> p (n t)").bitcast(I32))
        nc.sync.dma_start(d_tab[:], d_words[0].rearrange("p n t -> p (n t)").bitcast(I32))
        for h in range(2):
            nc.sync.dma_start(w_raw[h][:], w_rows[:, :, h * HALF : (h + 1) * HALF])

        ds_got = sb.tile([P, 2 * H], U8, name="ds_got", align_bytes=64)
        xs_got = sb.tile([P, S], U8, name="xs_got", tag="x_first", align_bytes=64)
        nc.vector.tensor_copy(ds_got[:, 0:H], ds_tab[:].indirect(k1_t[:]))
        nc.vector.tensor_copy(ds_got[:, H : 2 * H], ds_tab[:].indirect(k2_t[:]))
        nc.vector.tensor_copy(xs_got[:], xs_tab[:].indirect(offs_t[:]))
        planes = sb.tile([P, 2 * H + S], U8, name="planes", align_bytes=64)
        for a in range(2):
            nc.vector.tensor_copy(
                planes[:, a * H : (a + 1) * H].rearrange("p (t m) -> p t m", t=PACK),
                ds_got[:, a * H : (a + 1) * H].rearrange("p (m t) -> p t m", t=PACK),
            )
        nc.vector.tensor_copy(planes[:, 2 * H :].bitcast(I32), xs_got[:].bitcast(I32))
        for r in range(1, 4):
            nc.sync.dma_start(planes[r:P:32, :].bitcast(I32), planes[8 * r : P : 32, :].bitcast(I32))

        d_key = [sb.tile([P, H], U32, name="d_key%d" % a, align_bytes=64) for a in range(2)]
        w_bf = sb.tile([P, N * PACK], BF16, name="w_bf", align_bytes=64)
        w_s = sb.tile([P, N], U8, name="w_s", align_bytes=64)

        def pick_token_words(h, tag):
            got = sb.tile([P, HALF], U32, name="x_got%d" % h, tag=tag, align_bytes=64)
            nc.vector.tensor_copy(got[:], x_tab[:].bitcast(U32).indirect(offs_t[:, 16 * h : 16 * h + 16]))
            return got

        def pick_codes(a, lst):
            got = [sb.tile([P, HALF], U32, name="d_got%d_%d" % (a, h), tag="slot_d%d" % h, align_bytes=64) for h in range(2)]
            for h in range(2):
                nc.vector.tensor_copy(got[h][:], d_tab[:].bitcast(U32).indirect(lst[:, 16 * h : 16 * h + 16]))
            for h in range(2):
                nc.vector.tensor_copy(
                    d_key[a][:].rearrange("p (t m) -> p m t", t=PACK)[:, 64 * h : 64 * h + 64, :],
                    got[h][:].rearrange("p (m t) -> p m t", t=PACK),
                )

        def score(acc, t, a, h, start, stop):
            mm(acc, d_key[a][:, t * P : (t + 1) * P], planes[:, a * H + t * P : a * H + (t + 1) * P],
               x_got[h][:], planes[:, 2 * H + h * HALF : 2 * H + (h + 1) * HALF], start, stop)

        def cast_w(h):
            nc.scalar.copy(
                w_bf[:, h * HALF * PACK : (h + 1) * HALF * PACK].rearrange("p (c i t) -> p c t i", i=4, t=PACK),
                w_raw[h][:].rearrange("p t (c i) -> p c t i", i=4),
            )

        x_got = [pick_token_words(0, "x_first")]
        pick_codes(0, k1_t)
        cast_w(0)
        cast_w(1)

        lone_a = ps.tile([P, 2, HALF], F32, name="lone_a", tag="bank0")
        lone_b = ps.tile([P, 2, HALF], F32, name="lone_b", tag="bank1")
        early = [ps.tile([P, HALF], F32, name="early%d" % t, tag="bank%d" % (2 + t)) for t in range(2)]
        late = [ps.tile([P, 2, HALF], F32, name="late%d" % v, tag="bank%d" % (4 + v)) for v in range(2)]
        for t in range(2):
            score(lone_a[:, t, :], 2 + t, 0, 0, True, True)
        for t in range(2):
            score(early[t][:], t, 0, 0, True, False)
            score(early[t][:], t, 0, 0, False, False)
        a_sb = sb.tile([P, 2 * HALF], F32, name="a_sb", tag="slot_b", align_bytes=64)
        nc.scalar.copy(a_sb[:], lone_a[:].rearrange("p t n -> p (t n)"))

        pick_codes(1, k2_t)
        for t in range(2):
            score(lone_b[:, t, :], 2 + t, 1, 0, True, True)
        for t in range(2):
            score(early[t][:], t, 1, 0, False, True)
        x_got.append(pick_token_words(1, "slot_d0"))
        for t in range(PACK):
            score(late[t // 2][:, t % 2, :], t, 0, 1, True, False)
            score(late[t // 2][:, t % 2, :], t, 0, 1, False, False)
            score(late[t // 2][:, t % 2, :], t, 1, 1, False, True)

        s_sb = sb.tile([P, 2 * HALF], F32, name="s_sb", tag="slot_s", align_bytes=64)
        nc.vector.scalar_tensor_tensor(s_sb[:], lone_b[:].rearrange("p t n -> p (t n)"), 0.5, a_sb[:], MULT, ADD)
        w_q = sb.tile([P, N], U32, name="w_q", tag="slot_b", align_bytes=64)
        nc.vector.quantize_mx(out=w_q[:].bitcast(FP8X4), scales=w_s[:], in_=w_bf[:])

        sig0 = sb.tile([P, PACK, HALF], F32, name="sig0")
        for t in range(2):
            nc.scalar.activation(sig0[:, t, :], early[t][:], SIGMOID, scale=0.03125)
        nc.scalar.activation(sig0[:, 2:4, :].rearrange("p t n -> p (t n)"), s_sb[:], SIGMOID, scale=0.0625)
        sig1 = sb.tile([P, PACK, HALF], F32, name="sig1", tag="slot_s", align_bytes=64)
        for v in range(2):
            nc.scalar.activation(sig1[:, 2 * v : 2 * v + 2, :], late[v][:], SIGMOID, scale=0.03125)
        sig = [sig0, sig1]

        out_rows = out.rearrange("(u p) n -> p u n", p=P)
        gate = gn_t[:].unsqueeze(1).unsqueeze(3).to_broadcast([P, CHUNK // 4, PACK, 4])
        bank = 0
        for c in range(4):
            h, o = divmod(c * CHUNK, HALF)
            z_bf = sb.tile([P, CHUNK * PACK], BF16, name="z_bf%d" % c, tag="z_bf", bufs=2, align_bytes=64)
            nc.vector.tensor_tensor(
                z_bf[:].rearrange("p (c i t) -> p c t i", i=4, t=PACK),
                sig[h][:, :, o : o + CHUNK].rearrange("p t (c i) -> p c t i", i=4),
                gate,
                MULT,
            )
            z_q = sb.tile([P, CHUNK], U32, name="z_q%d" % c, align_bytes=64)
            z_s = sb.tile([P, CHUNK], U8, name="z_s%d" % c, align_bytes=64)
            nc.vector.quantize_mx(out=z_q[:].bitcast(FP8X4), scales=z_s[:], in_=z_bf[:])
            parts = 1 + h
            per = 4 // parts
            for part in range(parts):
                res = ps.tile([P, per, CHUNK], F32, name="res%d_%d" % (c, part), tag="bank%d" % bank)
                bank = bank + 1
                for v in range(per):
                    u = part * per + v
                    mm(res[:, v, :], w_q[:, u * P : (u + 1) * P], w_s[:, u * P : (u + 1) * P], z_q[:], z_s[:], True, True)
                res_sb = sb.tile([P, per, CHUNK], F32, name="res_sb%d_%d" % (c, part))
                dst = out_rows[:, part * per : (part + 1) * per, c * CHUNK : (c + 1) * CHUNK]
                if part == 0:
                    nc.scalar.copy(res_sb[:], res[:])
                    (nc.scalar if c == 3 else nc.sync).dma_start(dst, res_sb[:])
                else:
                    nc.vector.tensor_copy(res_sb[:], res[:])
                    nc.sync.dma_start(dst, res_sb[:])
